import numpy as np
CORES = [122,123,126,250,251,254,378,379,382,506,507,510]
N = 12
TK = 256
D = 128 * N
EPS = 0.01
def setup_inputs(rng):
    x = rng.standard_normal((N, 128, TK), dtype=np.float32) * (0.5 + np.abs(rng.standard_normal((1, 1, TK), dtype=np.float32))) + rng.standard_normal((1, 1, TK), dtype=np.float32)
    return {"x": x, "dy": rng.standard_normal((N, 128, TK), dtype=np.float32) + 0.5 * x + rng.standard_normal((1, 1, TK), dtype=np.float32)}
def setup_inputs_big(rng):
    d = setup_inputs(rng)
    for k in ("x", "dy"): d[k] = (d[k].astype(np.float32) * 1024.0).astype(d[k].dtype)
    return d
def setup_inputs_small(rng):
    d = setup_inputs(rng)
    for k in ("x", "dy"): d[k] = (d[k].astype(np.float32) * (1 / 1024.0)).astype(d[k].dtype)
    return d
def setup_inputs_apart(rng):
    d = setup_inputs(rng)
    f = (10.0 ** rng.permutation(np.linspace(-1.5, 1.5, N))).astype(np.float32).reshape(N, 1, 1)
    for k in ("x",): d[k] = (d[k].astype(np.float32) * f).astype(d[k].dtype)
    return d
def setup_inputs_mixed(rng):
    d = setup_inputs(rng)
    f = (10.0 ** rng.uniform(-3, 3, (1, 1, TK))).astype(np.float32); shape = rng.integers(3, size=(1, 1, TK))
    for k in ("x", "dy"):
        x = d[k].astype(np.float32)
        m = x.mean(axis=(0, 1), keepdims=True); level = m + np.sign(x - m) * np.abs(x - m).mean(axis=(0, 1), keepdims=True) * rng.uniform(0.9, 1.1, x.shape).astype(np.float32)
        other = x * np.where(rng.random(x.shape) < 0.5, 0.1, 1.0).astype(np.float32)
        d[k] = (np.where(shape == 1, level, np.where(shape == 2, other, x)) * f).astype(d[k].dtype)
    return d
def setup_inputs_offset(rng):
    d = setup_inputs(rng)
    x = d["x"]; spread = x.std(axis=(0, 1), keepdims=True)
    d["x"] = (x + spread * rng.uniform(16, 48, (1, 1, TK)) * rng.choice([-1.0, 1.0], (1, 1, TK))).astype(np.float32)
    return d
def reference(x, dy):
    X, DY = x.astype(np.float64), dy.astype(np.float64)
    mu = X.sum(axis=(0, 1)) / D
    rs = 1.0 / np.sqrt(((X - mu) ** 2).sum(axis=(0, 1)) / D + EPS)
    n = (X - mu) * rs
    a = DY.sum(axis=(0, 1)) / D; c = (DY * n).sum(axis=(0, 1)) / D
    return {"dx": (rs * (DY - a - n * c)).astype(np.float32)}

@@ -1,0 +1,247 @@
+import math
+from concourse.bass import DstId, RemoteDMATransfer
+from concourse.mybir import AluOpType, AxisListType, ActivationFunctionType
+
+N = 12
+D = 128 * N
+EPS = 0.01
+NSEM = 90
+
+SCRATCH = {
+    "xs": ("sbuf", [128, 256], "float32"),
+    "dys": ("sbuf", [128, 256], "float32"),
+    "ones": ("sbuf", [128, 128], "float32"),
+    "cd": ("sbuf", [128, 128], "float32"),
+    "ident": ("sbuf", [128, 128], "float32"),
+    "identd": ("sbuf", [128, 128], "float32"),
+    "G": ("sbuf", [128, N, 8], "float32"),
+    "urep": ("sbuf", [128, N, 2], "float32"),
+    "p2": ("sbuf", [128, N, 2], "float32"),
+    "t1": ("sbuf", [128, 6, 8], "float32"),
+    "t2": ("sbuf", [128, 3, 8], "float32"),
+    "t3": ("sbuf", [128, 8], "float32"),
+    "t4": ("sbuf", [128, 8], "float32"),
+    "sm": ("sbuf", [128, 80], "float32"),
+    "jq": ("sbuf", [128, 4, N], "float32"),
+    "junk": ("sbuf", [128, 6, 128], "float32"),
+    "xc": ("sbuf", [128, 256], "float32"),
+    "pr": ("sbuf", [128, 256], "float32"),
+    "tmp": ("sbuf", [128, 256], "float32"),
+    "w": ("sbuf", [128, 256], "float32"),
+    "dg": ("sbuf", [128, 256], "float32"),
+    "dxs": ("sbuf", [128, 256], "float32"),
+    "xT0": ("psum", [128, 512], "float32"),
+    "xT1": ("psum", [128, 512], "float32"),
+    "dT0": ("psum", [128, 512], "float32"),
+    "dT1": ("psum", [128, 512], "float32"),
+    "o0": ("psum", [128, 512], "float32"),
+    "o1": ("psum", [128, 512], "float32"),
+}
+SEMAPHORES = ["a1", "a2", "sent"] + ["s%d" % i for i in range(NSEM)]
+
+
+def _bits(m):
+    return bin(m).count("1")
+
+
+def rank_program(g, core, T, topo):
+    rank = T.rank_of(core)
+    if rank is None:
+        return
+    A, F = AluOpType, ActivationFunctionType
+    V, S, P, Y = g.vector, g.scalar, g.tensor, g.sync
+    G = T.G
+
+    cnt = [0]
+    events = []
+    seen = {}
+
+    def ev(instr, val=1):
+        e = (cnt[0], T.sem["s%d" % cnt[0]], val)
+        cnt[0] += 1
+        instr.then_inc(e[1], val)
+        events.append(e)
+        return e
+
+    def wait(qname, q, *es):
+        for e in es:
+            if (qname, e[0]) not in seen:
+                seen[(qname, e[0])] = True
+                seen[e[0]] = True
+                q.wait_ge(e[1], e[2])
+
+    def wv(*es): wait("v", V, *es)
+    def ws(*es): wait("s", S, *es)
+    def wp(*es): wait("p", P, *es)
+    def wy(*es): wait("y", Y, *es)
+    def wg(*es): wait("g", g, *es)
+
+    cores = list(T.cores)
+    my_host = topo.host(core)
+    chip_peers = [c for c in cores if c != core and topo.host(c) == my_host and topo.chip(c) == topo.chip(core)]
+    rack_peers = [c for c in cores if topo.host(c) != my_host and topo.rack(topo.host(c)) == topo.rack(my_host)]
+    pos = [c for c in cores if topo.host(c) == my_host].index(core)
+    far = [c for c in cores if topo.rack(topo.host(c)) != topo.rack(my_host) and topo.may_write(core, c)]
+    far_peer = far[pos]
+    rack_ranks = sorted(T.rank_of(c) for c in cores if topo.rack(topo.host(c)) == topo.rack(my_host))
+    lo, nr = rack_ranks[0], len(rack_ranks)
+    m_off = topo.mask(core, rack_peers[0]) & topo.mask(core, far_peer)
+    m_on = topo.mask(core, chip_peers[0]) & ~m_off
+
+    def bs(b):
+        return slice(b * 128, (b + 1) * 128)
+
+    def col(k):
+        return G[:, rank, k:k + 1]
+
+    def sm(k, n=2):
+        return T.sm[:, 4 * k:4 * k + n]
+
+    xT = [T.xT0[:, 0:128], T.xT1[:, 0:128]]
+    dT = [T.dT0[:, 0:128], T.dT1[:, 0:128]]
+    oP = [T.o0[:, 0:128], T.o1[:, 0:128]]
+
+    e_x = ev(Y.dma_start(T.xs[:], T.x[:]), 16)
+    e_dy = ev(S.dma_start(T.dys[:], T.dy[:]), 16)
+    e_ones = ev(V.memset(T.ones[:], 1.0))
+    e_cd = ev(V.memset(T.cd[:], float(D)))
+    e_z = ev(V.memset(T.urep[:], 0.0))
+    wg(e_ones)
+    e_id = ev(g.affine_select(T.ident[:], T.ones[:], [[-1, 128]], A.is_equal, 0.0, 0, 1))
+    wg(e_cd)
+    e_idd = ev(g.affine_select(T.identd[:], T.cd[:], [[-1, 128]], A.is_equal, 0.0, 0, 1))
+
+    e_xT, e_dT = [], []
+    for b in range(2):
+        wp(e_x, e_id)
+        e_xT.append(ev(P.transpose(xT[b], T.xs[:, bs(b)], T.ident[:])))
+    for b in range(2):
+        wp(e_dy)
+        e_dT.append(ev(P.transpose(dT[b], T.dys[:, bs(b)], T.ident[:])))
+
+    e_u, e_xc, e_m2, e_pr, e_c, e_sd = [], [], [], [], [], []
+    for b in range(2):
+        ws(e_xT[b])
+        e_u.append(ev(S.activation(T.junk[:, b, :], xT[b], F.Copy, scale=-1.0 / 128.0, accum_out=col(b))))
+        wv(e_xT[b], e_u[b])
+        e_xc.append(ev(V.tensor_scalar(T.xc[:, bs(b)], xT[b], col(b), None, A.add)))
+        ws(e_xc[b])
+        e_m2.append(ev(S.activation(T.junk[:, 2 + b, :], T.xc[:, bs(b)], F.Square, accum_out=col(2 + b))))
+    for b in range(2):
+        wv(e_dT[b], e_xc[b])
+        e_pr.append(ev(V.tensor_tensor(T.pr[:, bs(b)], T.xc[:, bs(b)], dT[b], A.mult)))
+        wv(e_pr[b])
+        e_c.append(ev(V.tensor_reduce(col(6 + b), T.pr[:, bs(b)], AxisListType.X, A.add)))
+        ws(e_dT[b], e_pr[b])
+        e_sd.append(ev(S.activation(T.junk[:, 4 + b, :], dT[b], F.Copy, accum_out=col(4 + b))))
+    own = e_u + e_m2 + e_sd + e_c
+
+    wg(*own)
+
+    def ids(cs):
+        out = []
+        for c in cs:
+            rid, pid = topo.addr(c, core)
+            out.append(DstId(rid=rid, pnc=pid))
+        return out
+
+    slot = G[:, rank, :]
+    g.remote_dma_fused([
+        RemoteDMATransfer(dst_ids=ids(rack_peers), dma_engine_mask=m_off, remote_sem=T.sem.a1,
+                          srcs=[slot], dsts=[slot for _ in rack_peers], alu_op=0),
+        RemoteDMATransfer(dst_ids=ids(chip_peers), dma_engine_mask=m_on, remote_sem=T.sem.a1,
+                          srcs=[slot], dsts=[slot for _ in chip_peers], alu_op=0),
+    ], local_sem=T.sem.sent)
+    n_a1 = len(rack_peers) * _bits(m_off) + len(chip_peers) * _bits(m_on)
+    n_sent = _bits(m_off) + _bits(m_on)
+
+    g.wait_ge(T.sem.a1, n_a1)
+    rid, pid = topo.addr(far_peer, core)
+    block = G[:, lo:lo + nr, :]
+    g.remote_dma(block, block, T.sem.a2, T.sem.sent, pid, rid, m_off)
+    n_sent += _bits(m_off)
+    n_a2 = _bits(m_off)
+
+    e_ur = []
+    for b in range(2):
+        wv(e_z, e_u[b])
+        e_ur.append(ev(V.tensor_scalar(T.urep[:, :, b], T.urep[:, :, b], col(b), None, A.add)))
+
+    wv(*own)
+    wv(*e_ur)
+    V.wait_ge(T.sem.a1, n_a1)
+    V.wait_ge(T.sem.a2, n_a2)
+    V.wait_ge(T.sem.sent, n_sent)
+    e_d = ev(V.tensor_tensor(G[:, :, 0:2], G[:, :, 0:2], T.urep[:], A.subtract))
+    wv(e_d)
+    e_p2 = ev(V.tensor_tensor(T.p2[:], G[:, :, 0:2], G[:, :, 4:6], A.mult))
+    e_t1 = ev(V.tensor_tensor(T.t1[:], G[:, 0:6, :], G[:, 6:12, :], A.add))
+    wv(e_t1)
+    e_t2 = ev(V.tensor_tensor(T.t2[:], T.t1[:, 0:3, :], T.t1[:, 3:6, :], A.add))
+    wv(e_t2)
+    e_t3 = ev(V.tensor_tensor(T.t3[:], T.t2[:, 0, :], T.t2[:, 1, :], A.add))
+    wv(e_t3)
+    e_t4 = ev(V.tensor_tensor(T.t4[:], T.t3[:], T.t2[:, 2, :], A.add))
+    Ds, SM, SD, SC = T.t4[:, 0:2], T.t4[:, 2:4], T.t4[:, 4:6], T.t4[:, 6:8]
+
+    ws(e_d)
+    e_q1 = [ev(S.activation(T.jq[:, b, :], G[:, :, b], F.Square, scale=math.sqrt(128.0),
+                            accum_out=T.sm[:, b:b + 1])) for b in range(2)]
+    ws(e_p2)
+    e_q2 = [ev(S.activation(T.jq[:, 2 + b, :], T.p2[:, :, b], F.Copy,
+                            accum_out=T.sm[:, 4 + b:5 + b])) for b in range(2)]
+    ws(e_t4)
+    e_t = ev(S.activation(sm(2), Ds, F.Square, scale=math.sqrt(128.0 / 12.0)))
+    wv(e_t4, *e_q1)
+    e_e1 = ev(V.tensor_tensor(sm(3), SM, sm(0), A.add))
+    wv(e_e1, e_t)
+    e_vr = ev(V.tensor_tensor(sm(4), sm(3), sm(2), A.subtract))
+    ws(e_vr)
+    e_sq = ev(S.activation(sm(5), sm(4), F.Sqrt, bias=EPS, scale=1.0 / D))
+
+    wv(e_vr)
+    e_vp = ev(V.tensor_scalar(sm(6), sm(4), float(D * EPS), None, A.add))
+    e_h = ev(V.tensor_scalar(sm(8), Ds, 1.0 / 12.0, None, A.mult))
+    wv(*e_q2)
+    e_k2 = ev(V.tensor_tensor(sm(10), sm(1), SC, A.subtract))
+    e_na = ev(V.tensor_scalar(sm(14), SD, -1.0 / D, None, A.mult))
+    wv(e_vp)
+    e_r2 = ev(V.reciprocal(sm(7), sm(6)))
+    wv(e_h)
+    e_k1 = ev(V.tensor_tensor(sm(9), sm(8), SD, A.mult))
+    wv(e_k1, e_k2)
+    e_nc = ev(V.tensor_tensor(sm(11), sm(10), sm(9), A.subtract))
+    wv(e_nc, e_r2)
+    e_be = ev(V.tensor_tensor(sm(12), sm(11), sm(7), A.mult))
+    wv(e_be)
+    e_g1 = ev(V.tensor_tensor(sm(13), sm(12), sm(8), A.mult))
+    wv(e_g1, e_na)
+    e_ga = ev(V.tensor_tensor(sm(15), sm(13), sm(14), A.add))
+    wv(e_ga)
+    e_w = []
+    for b in range(2):
+        e_a = ev(V.tensor_scalar(T.tmp[:, bs(b)], T.xc[:, bs(b)], T.sm[:, 48 + b:49 + b], T.sm[:, 60 + b:61 + b],
+                                 A.mult, A.add))
+        wv(e_a)
+        e_w.append(ev(V.tensor_tensor(T.w[:, bs(b)], T.tmp[:, bs(b)], dT[b], A.add)))
+    wv(e_sq, e_idd)
+    e_dg = [ev(V.tensor_scalar(T.dg[:, bs(b)], T.identd[:], T.sm[:, 20 + b:21 + b], T.sm[:, 28 + b:29 + b],
+                               A.mult, A.mult)) for b in range(2)]
+
+    e_o = []
+    for b in range(2):
+        wp(e_w[b], e_dg[b])
+        e_o.append(ev(P.matmul(oP[b], T.w[:, bs(b)], T.dg[:, bs(b)], True, True)))
+    wv(e_o[0])
+    e_c0 = ev(V.tensor_copy(T.dxs[:, bs(0)], oP[0]))
+    wy(e_c0)
+    e_s0 = ev(Y.dma_start(T.dx[:, bs(0)], T.dxs[:, bs(0)]), 16)
+    ws(e_o[1])
+    e_c1 = ev(S.activation(T.dxs[:, bs(1)], oP[1], F.Copy))
+    ws(e_c1)
+    e_s1 = ev(S.dma_start(T.dx[:, bs(1)], T.dxs[:, bs(1)]), 16)
+    wy(e_s0)
+    ws(e_s1)
+    for e in events:
+        if e[0] not in seen:
+            wg(e)

@@ -14,17 +14,21 @@ SCRATCH = {
     "cd": ("sbuf", [128, 128], "float32"),
     "ident": ("sbuf", [128, 128], "float32"),
     "identd": ("sbuf", [128, 128], "float32"),
-    "G": ("sbuf", [128, N, 8], "float32"),
+    "GX": ("sbuf", [128, N, 4], "float32"),
+    "GY": ("sbuf", [128, N, 4], "float32"),
     "urep": ("sbuf", [128, N, 2], "float32"),
+    "er": ("sbuf", [128, N, 2], "float32"),
     "p2": ("sbuf", [128, N, 2], "float32"),
-    "t1": ("sbuf", [128, 6, 8], "float32"),
-    "t2": ("sbuf", [128, 3, 8], "float32"),
-    "t3": ("sbuf", [128, 8], "float32"),
-    "t4": ("sbuf", [128, 8], "float32"),
+    "ee": ("sbuf", [128, N, 2], "float32"),
+    "t1": ("sbuf", [128, 6, 4], "float32"),
+    "t2": ("sbuf", [128, 3, 4], "float32"),
+    "t3": ("sbuf", [128, 4], "float32"),
+    "t4": ("sbuf", [128, 4], "float32"),
     "sm": ("sbuf", [128, 80], "float32"),
-    "jq": ("sbuf", [128, 4, N], "float32"),
+    "jq": ("sbuf", [128, 2, N], "float32"),
     "junk": ("sbuf", [128, 6, 128], "float32"),
     "xc": ("sbuf", [128, 256], "float32"),
+    "xh": ("sbuf", [128, 256], "float32"),
     "pr": ("sbuf", [128, 256], "float32"),
     "tmp": ("sbuf", [128, 256], "float32"),
     "w": ("sbuf", [128, 256], "float32"),
@@ -37,7 +41,7 @@ SCRATCH = {
     "o0": ("psum", [128, 512], "float32"),
     "o1": ("psum", [128, 512], "float32"),
 }
-SEMAPHORES = ["a1", "a2", "sent"] + ["s%d" % i for i in range(NSEM)]
+SEMAPHORES = ["ax1", "ax2", "ay1", "ay2", "sentx", "senty"] + ["s%d" % i for i in range(NSEM)]
 
 
 def _bits(m):
@@ -50,7 +54,7 @@ def rank_program(g, core, T, topo):
         return
     A, F = AluOpType, ActivationFunctionType
     V, S, P, Y = g.vector, g.scalar, g.tensor, g.sync
-    G = T.G
+    GX, GY = T.GX, T.GY
 
     cnt = [0]
     events = []
@@ -87,15 +91,39 @@ def rank_program(g, core, T, topo):
     lo, nr = rack_ranks[0], len(rack_ranks)
     m_off = topo.mask(core, rack_peers[0]) & topo.mask(core, far_peer)
     m_on = topo.mask(core, chip_peers[0]) & ~m_off
+    n_a1 = len(rack_peers) * _bits(m_off) + len(chip_peers) * _bits(m_on)
+    n_a2 = _bits(m_off)
+    n_sent = 2 * _bits(m_off) + _bits(m_on)
 
     def bs(b):
         return slice(b * 128, (b + 1) * 128)
 
-    def col(k):
-        return G[:, rank, k:k + 1]
-
     def sm(k, n=2):
         return T.sm[:, 4 * k:4 * k + n]
+
+    def smc(k, b):
+        return T.sm[:, 4 * k + b:4 * k + b + 1]
+
+    def ids(cs):
+        out = []
+        for c in cs:
+            rid, pid = topo.addr(c, core)
+            out.append(DstId(rid=rid, pnc=pid))
+        return out
+
+    def hop1(buf, arrive, sent):
+        slot = buf[:, rank, :]
+        g.remote_dma_fused([
+            RemoteDMATransfer(dst_ids=ids(rack_peers), dma_engine_mask=m_off, remote_sem=arrive,
+                              srcs=[slot], dsts=[slot for _ in rack_peers], alu_op=0),
+            RemoteDMATransfer(dst_ids=ids(chip_peers), dma_engine_mask=m_on, remote_sem=arrive,
+                              srcs=[slot], dsts=[slot for _ in chip_peers], alu_op=0),
+        ], local_sem=sent)
+
+    def hop2(buf, arrive, sent):
+        rid, pid = topo.addr(far_peer, core)
+        block = buf[:, lo:lo + nr, :]
+        g.remote_dma(block, block, arrive, sent, pid, rid, m_off)
 
     xT = [T.xT0[:, 0:128], T.xT1[:, 0:128]]
     dT = [T.dT0[:, 0:128], T.dT1[:, 0:128]]
@@ -122,74 +150,57 @@ def rank_program(g, core, T, topo):
     e_u, e_xc, e_m2, e_pr, e_c, e_sd = [], [], [], [], [], []
     for b in range(2):
         ws(e_xT[b])
-        e_u.append(ev(S.activation(T.junk[:, b, :], xT[b], F.Copy, scale=-1.0 / 128.0, accum_out=col(b))))
+        e_u.append(ev(S.activation(T.junk[:, b, :], xT[b], F.Copy, scale=-1.0 / 128.0,
+                                   accum_out=GX[:, rank, b:b + 1])))
         wv(e_xT[b], e_u[b])
-        e_xc.append(ev(V.tensor_scalar(T.xc[:, bs(b)], xT[b], col(b), None, A.add)))
+        e_xc.append(ev(V.tensor_scalar(T.xc[:, bs(b)], xT[b], GX[:, rank, b:b + 1], None, A.add)))
         ws(e_xc[b])
-        e_m2.append(ev(S.activation(T.junk[:, 2 + b, :], T.xc[:, bs(b)], F.Square, accum_out=col(2 + b))))
+        e_m2.append(ev(S.activation(T.junk[:, 2 + b, :], T.xc[:, bs(b)], F.Square,
+                                    accum_out=GX[:, rank, 2 + b:3 + b])))
     for b in range(2):
         wv(e_dT[b], e_xc[b])
         e_pr.append(ev(V.tensor_tensor(T.pr[:, bs(b)], T.xc[:, bs(b)], dT[b], A.mult)))
         wv(e_pr[b])
-        e_c.append(ev(V.tensor_reduce(col(6 + b), T.pr[:, bs(b)], AxisListType.X, A.add)))
+        e_c.append(ev(V.tensor_reduce(GY[:, rank, 2 + b:3 + b], T.pr[:, bs(b)], AxisListType.X, A.add)))
         ws(e_dT[b], e_pr[b])
-        e_sd.append(ev(S.activation(T.junk[:, 4 + b, :], dT[b], F.Copy, accum_out=col(4 + b))))
-    own = e_u + e_m2 + e_sd + e_c
+        e_sd.append(ev(S.activation(T.junk[:, 4 + b, :], dT[b], F.Copy, scale=1.0 / D,
+                                    accum_out=GY[:, rank, b:b + 1])))
+    ownx = e_u + e_m2
+    owny = e_sd + e_c
 
-    wg(*own)
-
-    def ids(cs):
-        out = []
-        for c in cs:
-            rid, pid = topo.addr(c, core)
-            out.append(DstId(rid=rid, pnc=pid))
-        return out
-
-    slot = G[:, rank, :]
-    g.remote_dma_fused([
-        RemoteDMATransfer(dst_ids=ids(rack_peers), dma_engine_mask=m_off, remote_sem=T.sem.a1,
-                          srcs=[slot], dsts=[slot for _ in rack_peers], alu_op=0),
-        RemoteDMATransfer(dst_ids=ids(chip_peers), dma_engine_mask=m_on, remote_sem=T.sem.a1,
-                          srcs=[slot], dsts=[slot for _ in chip_peers], alu_op=0),
-    ], local_sem=T.sem.sent)
-    n_a1 = len(rack_peers) * _bits(m_off) + len(chip_peers) * _bits(m_on)
-    n_sent = _bits(m_off) + _bits(m_on)
-
-    g.wait_ge(T.sem.a1, n_a1)
-    rid, pid = topo.addr(far_peer, core)
-    block = G[:, lo:lo + nr, :]
-    g.remote_dma(block, block, T.sem.a2, T.sem.sent, pid, rid, m_off)
-    n_sent += _bits(m_off)
-    n_a2 = _bits(m_off)
+    wg(*ownx)
+    hop1(GX, T.sem.ax1, T.sem.sentx)
+    wg(*owny)
+    hop1(GY, T.sem.ay1, T.sem.senty)
+    g.wait_ge(T.sem.ax1, n_a1)
+    hop2(GX, T.sem.ax2, T.sem.sentx)
+    g.wait_ge(T.sem.ay1, n_a1)
+    hop2(GY, T.sem.ay2, T.sem.senty)
 
     e_ur = []
     for b in range(2):
         wv(e_z, e_u[b])
-        e_ur.append(ev(V.tensor_scalar(T.urep[:, :, b], T.urep[:, :, b], col(b), None, A.add)))
+        e_ur.append(ev(V.tensor_scalar(T.urep[:, :, b], T.urep[:, :, b], GX[:, rank, b:b + 1], None, A.add)))
 
-    wv(*own)
+    wv(*ownx)
     wv(*e_ur)
-    V.wait_ge(T.sem.a1, n_a1)
-    V.wait_ge(T.sem.a2, n_a2)
-    V.wait_ge(T.sem.sent, n_sent)
-    e_d = ev(V.tensor_tensor(G[:, :, 0:2], G[:, :, 0:2], T.urep[:], A.subtract))
+    V.wait_ge(T.sem.ax1, n_a1)
+    V.wait_ge(T.sem.ax2, n_a2)
+    V.wait_ge(T.sem.sentx, n_sent)
+    e_d = ev(V.tensor_tensor(GX[:, :, 0:2], GX[:, :, 0:2], T.urep[:], A.subtract))
     wv(e_d)
-    e_p2 = ev(V.tensor_tensor(T.p2[:], G[:, :, 0:2], G[:, :, 4:6], A.mult))
-    e_t1 = ev(V.tensor_tensor(T.t1[:], G[:, 0:6, :], G[:, 6:12, :], A.add))
+    e_t1 = ev(V.tensor_tensor(T.t1[:], GX[:, 0:6, :], GX[:, 6:12, :], A.add))
     wv(e_t1)
     e_t2 = ev(V.tensor_tensor(T.t2[:], T.t1[:, 0:3, :], T.t1[:, 3:6, :], A.add))
     wv(e_t2)
     e_t3 = ev(V.tensor_tensor(T.t3[:], T.t2[:, 0, :], T.t2[:, 1, :], A.add))
     wv(e_t3)
     e_t4 = ev(V.tensor_tensor(T.t4[:], T.t3[:], T.t2[:, 2, :], A.add))
-    Ds, SM, SD, SC = T.t4[:, 0:2], T.t4[:, 2:4], T.t4[:, 4:6], T.t4[:, 6:8]
+    Ds, SM = T.t4[:, 0:2], T.t4[:, 2:4]
 
     ws(e_d)
-    e_q1 = [ev(S.activation(T.jq[:, b, :], G[:, :, b], F.Square, scale=math.sqrt(128.0),
-                            accum_out=T.sm[:, b:b + 1])) for b in range(2)]
-    ws(e_p2)
-    e_q2 = [ev(S.activation(T.jq[:, 2 + b, :], T.p2[:, :, b], F.Copy,
-                            accum_out=T.sm[:, 4 + b:5 + b])) for b in range(2)]
+    e_q1 = [ev(S.activation(T.jq[:, b, :], GX[:, :, b], F.Square, scale=math.sqrt(128.0),
+                            accum_out=smc(0, b))) for b in range(2)]
     ws(e_t4)
     e_t = ev(S.activation(sm(2), Ds, F.Square, scale=math.sqrt(128.0 / 12.0)))
     wv(e_t4, *e_q1)
@@ -202,31 +213,37 @@ def rank_program(g, core, T, topo):
     wv(e_vr)
     e_vp = ev(V.tensor_scalar(sm(6), sm(4), float(D * EPS), None, A.add))
     e_h = ev(V.tensor_scalar(sm(8), Ds, 1.0 / 12.0, None, A.mult))
-    wv(*e_q2)
-    e_k2 = ev(V.tensor_tensor(sm(10), sm(1), SC, A.subtract))
-    e_na = ev(V.tensor_scalar(sm(14), SD, -1.0 / D, None, A.mult))
     wv(e_vp)
     e_r2 = ev(V.reciprocal(sm(7), sm(6)))
     wv(e_h)
-    e_k1 = ev(V.tensor_tensor(sm(9), sm(8), SD, A.mult))
-    wv(e_k1, e_k2)
-    e_nc = ev(V.tensor_tensor(sm(11), sm(10), sm(9), A.subtract))
-    wv(e_nc, e_r2)
-    e_be = ev(V.tensor_tensor(sm(12), sm(11), sm(7), A.mult))
-    wv(e_be)
-    e_g1 = ev(V.tensor_tensor(sm(13), sm(12), sm(8), A.mult))
-    wv(e_g1, e_na)
-    e_ga = ev(V.tensor_tensor(sm(15), sm(13), sm(14), A.add))
-    wv(e_ga)
-    e_w = []
+    e_er = [ev(V.tensor_scalar(T.er[:, :, b], GX[:, :, b], smc(8, b), float(-D), A.subtract, A.mult))
+            for b in range(2)]
+    e_xh = [ev(V.tensor_scalar(T.xh[:, bs(b)], T.xc[:, bs(b)], smc(8, b), None, A.add)) for b in range(2)]
+    wv(e_r2)
+    e_nr = ev(V.tensor_scalar(sm(9), sm(7), -1.0, None, A.mult))
+
+    wv(*owny)
+    wv(*e_er)
+    wv(*e_xh)
+    wv(e_nr)
+    V.wait_ge(T.sem.ay1, n_a1)
+    V.wait_ge(T.sem.ay2, n_a2)
+    e_p2 = ev(V.tensor_tensor(T.p2[:], T.er[:], GY[:, :, 0:2], A.mult))
+    wv(e_p2)
+    e_ee = ev(V.tensor_tensor(T.ee[:], T.p2[:], GY[:, :, 2:4], A.add))
+    wv(e_ee)
+    e_w, e_dg = [], []
     for b in range(2):
-        e_a = ev(V.tensor_scalar(T.tmp[:, bs(b)], T.xc[:, bs(b)], T.sm[:, 48 + b:49 + b], T.sm[:, 60 + b:61 + b],
-                                 A.mult, A.add))
+        e_cv = ev(V.tensor_reduce(smc(10, b), T.ee[:, :, b], AxisListType.X, A.add))
+        e_na = ev(V.tensor_reduce(smc(11, b), GY[:, :, b], AxisListType.X, A.add, negate=True))
+        wv(e_cv)
+        e_be = ev(V.tensor_tensor(smc(12, b), smc(10, b), smc(9, b), A.mult))
+        wv(e_be, e_na)
+        e_a = ev(V.tensor_scalar(T.tmp[:, bs(b)], T.xh[:, bs(b)], smc(12, b), smc(11, b), A.mult, A.add))
         wv(e_a)
         e_w.append(ev(V.tensor_tensor(T.w[:, bs(b)], T.tmp[:, bs(b)], dT[b], A.add)))
-    wv(e_sq, e_idd)
-    e_dg = [ev(V.tensor_scalar(T.dg[:, bs(b)], T.identd[:], T.sm[:, 20 + b:21 + b], T.sm[:, 28 + b:29 + b],
-                               A.mult, A.mult)) for b in range(2)]
+        wv(e_sq, e_idd)
+        e_dg.append(ev(V.tensor_scalar(T.dg[:, bs(b)], T.identd[:], smc(5, b), smc(7, b), A.mult, A.mult)))
 
     e_o = []
     for b in range(2):
@@ -242,6 +259,7 @@ def rank_program(g, core, T, topo):
     e_s1 = ev(S.dma_start(T.dx[:, bs(1)], T.dxs[:, bs(1)]), 16)
     wy(e_s0)
     ws(e_s1)
+    g.wait_ge(T.sem.senty, n_sent)
     for e in events:
         if e[0] not in seen:
             wg(e)

@@ -11,21 +11,19 @@ SCRATCH = {
     "xs": ("sbuf", [128, 256], "float32"),
     "dys": ("sbuf", [128, 256], "float32"),
     "ones": ("sbuf", [128, 128], "float32"),
-    "cd": ("sbuf", [128, 128], "float32"),
     "ident": ("sbuf", [128, 128], "float32"),
-    "identd": ("sbuf", [128, 128], "float32"),
     "GX": ("sbuf", [128, N, 4], "float32"),
     "GY": ("sbuf", [128, N, 4], "float32"),
     "urep": ("sbuf", [128, N, 2], "float32"),
     "er": ("sbuf", [128, N, 2], "float32"),
     "p2": ("sbuf", [128, N, 2], "float32"),
-    "ee": ("sbuf", [128, N, 2], "float32"),
+    "sc": ("sbuf", [128, 2, N], "float32"),
     "t1": ("sbuf", [128, 6, 4], "float32"),
     "t2": ("sbuf", [128, 3, 4], "float32"),
     "t3": ("sbuf", [128, 4], "float32"),
     "t4": ("sbuf", [128, 4], "float32"),
     "sm": ("sbuf", [128, 80], "float32"),
-    "jq": ("sbuf", [128, 2, N], "float32"),
+    "jq": ("sbuf", [128, 4, N], "float32"),
     "junk": ("sbuf", [128, 6, 128], "float32"),
     "xc": ("sbuf", [128, 256], "float32"),
     "xh": ("sbuf", [128, 256], "float32"),
@@ -40,6 +38,7 @@ SCRATCH = {
     "dT1": ("psum", [128, 512], "float32"),
     "o0": ("psum", [128, 512], "float32"),
     "o1": ("psum", [128, 512], "float32"),
+    "o2": ("psum", [128, 512], "float32"),
 }
 SEMAPHORES = ["ax1", "ax2", "ay1", "ay2", "sentx", "senty"] + ["s%d" % i for i in range(NSEM)]
 
@@ -84,15 +83,23 @@ def rank_program(g, core, T, topo):
     my_host = topo.host(core)
     chip_peers = [c for c in cores if c != core and topo.host(c) == my_host and topo.chip(c) == topo.chip(core)]
     rack_peers = [c for c in cores if topo.host(c) != my_host and topo.rack(topo.host(c)) == topo.rack(my_host)]
-    pos = [c for c in cores if topo.host(c) == my_host].index(core)
-    far = [c for c in cores if topo.rack(topo.host(c)) != topo.rack(my_host) and topo.may_write(core, c)]
-    far_peer = far[pos]
-    rack_ranks = sorted(T.rank_of(c) for c in cores if topo.rack(topo.host(c)) == topo.rack(my_host))
-    lo, nr = rack_ranks[0], len(rack_ranks)
+
+    def far_of(c):
+        pos = [k for k in cores if topo.host(k) == topo.host(c)].index(c)
+        return [k for k in cores if topo.rack(topo.host(k)) != topo.rack(topo.host(c)) and topo.may_write(c, k)][pos]
+
+    far_peer = far_of(core)
+    order = []
+    for c in cores:
+        if c not in order:
+            order.append(c)
+            order.append(far_of(c))
+    me = order.index(core)
+    lo = min(me, order.index(far_peer))
     m_off = topo.mask(core, rack_peers[0]) & topo.mask(core, far_peer)
     m_on = topo.mask(core, chip_peers[0]) & ~m_off
-    n_a1 = len(rack_peers) * _bits(m_off) + len(chip_peers) * _bits(m_on)
-    n_a2 = _bits(m_off)
+    n_a1 = _bits(m_off)
+    n_a2 = len(rack_peers) * _bits(m_off) + len(chip_peers) * _bits(m_on)
     n_sent = 2 * _bits(m_off) + _bits(m_on)
 
     def bs(b):
@@ -112,32 +119,28 @@ def rank_program(g, core, T, topo):
         return out
 
     def hop1(buf, arrive, sent):
-        slot = buf[:, rank, :]
-        g.remote_dma_fused([
-            RemoteDMATransfer(dst_ids=ids(rack_peers), dma_engine_mask=m_off, remote_sem=arrive,
-                              srcs=[slot], dsts=[slot for _ in rack_peers], alu_op=0),
-            RemoteDMATransfer(dst_ids=ids(chip_peers), dma_engine_mask=m_on, remote_sem=arrive,
-                              srcs=[slot], dsts=[slot for _ in chip_peers], alu_op=0),
-        ], local_sem=sent)
+        rid, pid = topo.addr(far_peer, core)
+        slot = buf[:, me, :]
+        g.remote_dma(slot, slot, arrive, sent, pid, rid, m_off)
 
     def hop2(buf, arrive, sent):
-        rid, pid = topo.addr(far_peer, core)
-        block = buf[:, lo:lo + nr, :]
-        g.remote_dma(block, block, arrive, sent, pid, rid, m_off)
+        pair = buf[:, lo:lo + 2, :]
+        g.remote_dma_fused([
+            RemoteDMATransfer(dst_ids=ids(rack_peers), dma_engine_mask=m_off, remote_sem=arrive,
+                              srcs=[pair], dsts=[pair for _ in rack_peers], alu_op=0),
+            RemoteDMATransfer(dst_ids=ids(chip_peers), dma_engine_mask=m_on, remote_sem=arrive,
+                              srcs=[pair], dsts=[pair for _ in chip_peers], alu_op=0),
+        ], local_sem=sent)
 
     xT = [T.xT0[:, 0:128], T.xT1[:, 0:128]]
     dT = [T.dT0[:, 0:128], T.dT1[:, 0:128]]
-    oP = [T.o0[:, 0:128], T.o1[:, 0:128]]
 
     e_x = ev(Y.dma_start(T.xs[:], T.x[:]), 16)
     e_dy = ev(S.dma_start(T.dys[:], T.dy[:]), 16)
     e_ones = ev(V.memset(T.ones[:], 1.0))
-    e_cd = ev(V.memset(T.cd[:], float(D)))
     e_z = ev(V.memset(T.urep[:], 0.0))
     wg(e_ones)
     e_id = ev(g.affine_select(T.ident[:], T.ones[:], [[-1, 128]], A.is_equal, 0.0, 0, 1))
-    wg(e_cd)
-    e_idd = ev(g.affine_select(T.identd[:], T.cd[:], [[-1, 128]], A.is_equal, 0.0, 0, 1))
 
     e_xT, e_dT = [], []
     for b in range(2):
@@ -151,20 +154,20 @@ def rank_program(g, core, T, topo):
     for b in range(2):
         ws(e_xT[b])
         e_u.append(ev(S.activation(T.junk[:, b, :], xT[b], F.Copy, scale=-1.0 / 128.0,
-                                   accum_out=GX[:, rank, b:b + 1])))
+                                   accum_out=GX[:, me, b:b + 1])))
         wv(e_xT[b], e_u[b])
-        e_xc.append(ev(V.tensor_scalar(T.xc[:, bs(b)], xT[b], GX[:, rank, b:b + 1], None, A.add)))
+        e_xc.append(ev(V.tensor_scalar(T.xc[:, bs(b)], xT[b], GX[:, me, b:b + 1], None, A.add)))
         ws(e_xc[b])
         e_m2.append(ev(S.activation(T.junk[:, 2 + b, :], T.xc[:, bs(b)], F.Square,
-                                    accum_out=GX[:, rank, 2 + b:3 + b])))
+                                    accum_out=GX[:, me, 2 + b:3 + b])))
     for b in range(2):
         wv(e_dT[b], e_xc[b])
         e_pr.append(ev(V.tensor_tensor(T.pr[:, bs(b)], T.xc[:, bs(b)], dT[b], A.mult)))
         wv(e_pr[b])
-        e_c.append(ev(V.tensor_reduce(GY[:, rank, 2 + b:3 + b], T.pr[:, bs(b)], AxisListType.X, A.add)))
+        e_c.append(ev(V.tensor_reduce(GY[:, me, 2 + b:3 + b], T.pr[:, bs(b)], AxisListType.X, A.add, negate=True)))
         ws(e_dT[b], e_pr[b])
         e_sd.append(ev(S.activation(T.junk[:, 4 + b, :], dT[b], F.Copy, scale=1.0 / D,
-                                    accum_out=GY[:, rank, b:b + 1])))
+                                    accum_out=GY[:, me, b:b + 1])))
     ownx = e_u + e_m2
     owny = e_sd + e_c
 
@@ -180,7 +183,15 @@ def rank_program(g, core, T, topo):
     e_ur = []
     for b in range(2):
         wv(e_z, e_u[b])
-        e_ur.append(ev(V.tensor_scalar(T.urep[:, :, b], T.urep[:, :, b], GX[:, rank, b:b + 1], None, A.add)))
+        e_ur.append(ev(V.tensor_scalar(T.urep[:, :, b], T.urep[:, :, b], GX[:, me, b:b + 1], None, A.add)))
+    wv(*e_m2)
+    e_vo = ev(V.tensor_scalar(sm(13), GX[:, me, 2:4], float(D * EPS), None, A.add))
+    ws(e_vo)
+    e_pd = ev(S.activation(sm(16), sm(13), F.Sqrt, scale=float(D)))
+    wv(e_vo)
+    e_ri = ev(V.reciprocal(sm(14), sm(13)))
+    wv(e_ri)
+    e_bc = ev(V.tensor_scalar(sm(15), sm(14), float(D * EPS), None, A.mult))
 
     wv(*ownx)
     wv(*e_ur)
@@ -197,68 +208,86 @@ def rank_program(g, core, T, topo):
     wv(e_t3)
     e_t4 = ev(V.tensor_tensor(T.t4[:], T.t3[:], T.t2[:, 2, :], A.add))
     Ds, SM = T.t4[:, 0:2], T.t4[:, 2:4]
+    wv(e_t4)
+    e_nh = ev(V.tensor_scalar(sm(9), Ds, -float(D) / 12.0, None, A.mult))
+    e_h = ev(V.tensor_scalar(sm(8), Ds, 1.0 / 12.0, None, A.mult))
 
     ws(e_d)
     e_q1 = [ev(S.activation(T.jq[:, b, :], GX[:, :, b], F.Square, scale=math.sqrt(128.0),
                             accum_out=smc(0, b))) for b in range(2)]
     ws(e_t4)
     e_t = ev(S.activation(sm(2), Ds, F.Square, scale=math.sqrt(128.0 / 12.0)))
-    wv(e_t4, *e_q1)
+    wv(*e_q1)
     e_e1 = ev(V.tensor_tensor(sm(3), SM, sm(0), A.add))
     wv(e_e1, e_t)
     e_vr = ev(V.tensor_tensor(sm(4), sm(3), sm(2), A.subtract))
-    ws(e_vr)
-    e_sq = ev(S.activation(sm(5), sm(4), F.Sqrt, bias=EPS, scale=1.0 / D))
-
     wv(e_vr)
     e_vp = ev(V.tensor_scalar(sm(6), sm(4), float(D * EPS), None, A.add))
-    e_h = ev(V.tensor_scalar(sm(8), Ds, 1.0 / 12.0, None, A.mult))
     wv(e_vp)
     e_r2 = ev(V.reciprocal(sm(7), sm(6)))
-    wv(e_h)
-    e_er = [ev(V.tensor_scalar(T.er[:, :, b], GX[:, :, b], smc(8, b), float(-D), A.subtract, A.mult))
+    wv(e_r2, e_pd)
+    e_a1 = ev(V.tensor_tensor(sm(17), sm(16), sm(7), A.mult))
+
+    ws(e_nh)
+    e_er = [ev(S.activation(T.er[:, :, b], GX[:, :, b], F.Identity, bias=smc(9, b), scale=float(D)))
             for b in range(2)]
-    e_xh = [ev(V.tensor_scalar(T.xh[:, bs(b)], T.xc[:, bs(b)], smc(8, b), None, A.add)) for b in range(2)]
-    wv(e_r2)
-    e_nr = ev(V.tensor_scalar(sm(9), sm(7), -1.0, None, A.mult))
+    ws(e_h)
+    e_xh = [ev(S.activation(T.xh[:, bs(b)], T.xc[:, bs(b)], F.Identity, bias=smc(8, b))) for b in range(2)]
+    ws(e_vr, e_ri, e_bc)
+    e_sq = [ev(S.activation(smc(5, b), smc(4, b), F.Sqrt, bias=smc(15, b), scale=smc(14, b)))
+            for b in range(2)]
+
+    def diag(b):
+        ws(e_a1, e_sq[b])
+        e_rs = ev(S.activation(smc(18, b), smc(5, b), F.Identity, scale=smc(17, b)))
+        ws(e_rs, e_id)
+        return ev(S.activation(T.dg[:, bs(b)], T.ident[:], F.Identity, scale=smc(18, b)))
+
+    e_dg = [diag(0)]
+    ws(*owny)
+    S.wait_ge(T.sem.ay1, n_a1)
+    S.wait_ge(T.sem.ay2, n_a2)
+    e_dn = []
+    for b in range(2):
+        e_na = ev(S.activation(T.jq[:, 2 + b, :], GY[:, :, b], F.Copy, scale=-1.0, accum_out=smc(11, b)))
+        ws(e_na, e_pr[b])
+        e_dn.append(ev(S.activation(dT[b], dT[b], F.Identity, bias=smc(11, b))))
+    e_dg.append(diag(1))
 
     wv(*owny)
     wv(*e_er)
-    wv(*e_xh)
-    wv(e_nr)
     V.wait_ge(T.sem.ay1, n_a1)
     V.wait_ge(T.sem.ay2, n_a2)
     e_p2 = ev(V.tensor_tensor(T.p2[:], T.er[:], GY[:, :, 0:2], A.mult))
     wv(e_p2)
-    e_ee = ev(V.tensor_tensor(T.ee[:], T.p2[:], GY[:, :, 2:4], A.add))
-    wv(e_ee)
-    e_w, e_dg = [], []
+    e_w = []
     for b in range(2):
-        e_cv = ev(V.tensor_reduce(smc(10, b), T.ee[:, :, b], AxisListType.X, A.add))
-        e_na = ev(V.tensor_reduce(smc(11, b), GY[:, :, b], AxisListType.X, A.add, negate=True))
-        wv(e_cv)
-        e_be = ev(V.tensor_tensor(smc(12, b), smc(10, b), smc(9, b), A.mult))
-        wv(e_be, e_na)
-        e_a = ev(V.tensor_scalar(T.tmp[:, bs(b)], T.xh[:, bs(b)], smc(12, b), smc(11, b), A.mult, A.add))
-        wv(e_a)
+        e_cv = ev(V.tensor_tensor_scan(T.sc[:, b, :], T.p2[:, :, b], GY[:, :, 2 + b], 0.0, A.add, A.add))
+        wv(e_cv, e_xh[b])
+        e_a = ev(V.tensor_scalar(T.tmp[:, bs(b)], T.xh[:, bs(b)], smc(7, b), T.sc[:, b, N - 1:N],
+                                 A.mult, A.mult))
+        wv(e_a, e_dn[b])
         e_w.append(ev(V.tensor_tensor(T.w[:, bs(b)], T.tmp[:, bs(b)], dT[b], A.add)))
-        wv(e_sq, e_idd)
-        e_dg.append(ev(V.tensor_scalar(T.dg[:, bs(b)], T.identd[:], smc(5, b), smc(7, b), A.mult, A.mult)))
 
+    pieces = [(0, T.o0, 0, 128), (1, T.o1, 128, 64), (1, T.o2, 192, 64)]
     e_o = []
-    for b in range(2):
+    for b, ob, c0, n in pieces:
         wp(e_w[b], e_dg[b])
-        e_o.append(ev(P.matmul(oP[b], T.w[:, bs(b)], T.dg[:, bs(b)], True, True)))
-    wv(e_o[0])
-    e_c0 = ev(V.tensor_copy(T.dxs[:, bs(0)], oP[0]))
-    wy(e_c0)
-    e_s0 = ev(Y.dma_start(T.dx[:, bs(0)], T.dxs[:, bs(0)]), 16)
-    ws(e_o[1])
-    e_c1 = ev(S.activation(T.dxs[:, bs(1)], oP[1], F.Copy))
-    ws(e_c1)
-    e_s1 = ev(S.dma_start(T.dx[:, bs(1)], T.dxs[:, bs(1)]), 16)
-    wy(e_s0)
-    ws(e_s1)
+        e_o.append(ev(P.matmul(ob[:, 0:n], T.w[:, bs(b)], T.dg[:, c0:c0 + n], True, True)))
+    e_st = []
+    for k in range(2):
+        b, ob, c0, n = pieces[k]
+        wv(e_o[k])
+        e_cp = ev(V.tensor_copy(T.dxs[:, c0:c0 + n], ob[:, 0:n]))
+        wy(e_cp)
+        e_st.append(ev(Y.dma_start(T.dx[:, c0:c0 + n], T.dxs[:, c0:c0 + n]), 16))
+    b, ob, c0, n = pieces[2]
+    ws(e_o[2])
+    e_cp = ev(S.activation(T.dxs[:, c0:c0 + n], ob[:, 0:n], F.Copy))
+    ws(e_cp)
+    e_s2 = ev(S.dma_start(T.dx[:, c0:c0 + n], T.dxs[:, c0:c0 + n]), 16)
+    wy(*e_st)
+    ws(e_s2)
     g.wait_ge(T.sem.senty, n_sent)
     for e in events:
         if e[0] not in seen:

@@ -22,7 +22,7 @@ SCRATCH = {
     "t2": ("sbuf", [128, 3, 4], "float32"),
     "t3": ("sbuf", [128, 4], "float32"),
     "t4": ("sbuf", [128, 4], "float32"),
-    "sm": ("sbuf", [128, 80], "float32"),
+    "sm": ("sbuf", [128, 88], "float32"),
     "jq": ("sbuf", [128, 4, N], "float32"),
     "junk": ("sbuf", [128, 6, 128], "float32"),
     "xc": ("sbuf", [128, 256], "float32"),
@@ -155,19 +155,18 @@ def rank_program(g, core, T, topo):
         ws(e_xT[b])
         e_u.append(ev(S.activation(T.junk[:, b, :], xT[b], F.Copy, scale=-1.0 / 128.0,
                                    accum_out=GX[:, me, b:b + 1])))
-        wv(e_xT[b], e_u[b])
-        e_xc.append(ev(V.tensor_scalar(T.xc[:, bs(b)], xT[b], GX[:, me, b:b + 1], None, A.add)))
-        ws(e_xc[b])
-        e_m2.append(ev(S.activation(T.junk[:, 2 + b, :], T.xc[:, bs(b)], F.Square,
+        ws(e_u[b])
+        e_m2.append(ev(S.activation(T.junk[:, 2 + b, :], xT[b], F.Square, bias=GX[:, me, b:b + 1],
                                     accum_out=GX[:, me, 2 + b:3 + b])))
+        wv(e_xT[b], e_u[b], e_m2[b])
+        e_xc.append(ev(V.tensor_scalar(T.xc[:, bs(b)], xT[b], GX[:, me, b:b + 1], None, A.add)))
     for b in range(2):
         wv(e_dT[b], e_xc[b])
         e_pr.append(ev(V.tensor_tensor(T.pr[:, bs(b)], T.xc[:, bs(b)], dT[b], A.mult)))
         wv(e_pr[b])
-        e_c.append(ev(V.tensor_reduce(GY[:, me, 2 + b:3 + b], T.pr[:, bs(b)], AxisListType.X, A.add, negate=True)))
+        e_c.append(ev(V.tensor_reduce(GY[:, me, 2 + b:3 + b], T.pr[:, bs(b)], AxisListType.X, A.add)))
         ws(e_dT[b], e_pr[b])
-        e_sd.append(ev(S.activation(T.junk[:, 4 + b, :], dT[b], F.Copy, scale=1.0 / D,
-                                    accum_out=GY[:, me, b:b + 1])))
+        e_sd.append(ev(S.activation(T.junk[:, 4 + b, :], dT[b], F.Copy, accum_out=GY[:, me, b:b + 1])))
     ownx = e_u + e_m2
     owny = e_sd + e_c
 
@@ -191,13 +190,17 @@ def rank_program(g, core, T, topo):
     wv(e_vo)
     e_ri = ev(V.reciprocal(sm(14), sm(13)))
     wv(e_ri)
-    e_bc = ev(V.tensor_scalar(sm(15), sm(14), float(D * EPS), None, A.mult))
+    e_nri = ev(V.tensor_scalar(sm(15), sm(14), -1.0, None, A.mult))
+    wv(e_pd)
+    e_pdn = ev(V.tensor_scalar(sm(19), sm(16), -1.0, None, A.mult))
+    V.wait_ge(T.sem.sentx, n_sent)
+    e_own = ev(V.tensor_copy(GX[:, me, 2:4], sm(13)))
 
     wv(*ownx)
     wv(*e_ur)
+    wv(e_own)
     V.wait_ge(T.sem.ax1, n_a1)
     V.wait_ge(T.sem.ax2, n_a2)
-    V.wait_ge(T.sem.sentx, n_sent)
     e_d = ev(V.tensor_tensor(GX[:, :, 0:2], GX[:, :, 0:2], T.urep[:], A.subtract))
     wv(e_d)
     e_t1 = ev(V.tensor_tensor(T.t1[:], GX[:, 0:6, :], GX[:, 6:12, :], A.add))
@@ -209,7 +212,6 @@ def rank_program(g, core, T, topo):
     e_t4 = ev(V.tensor_tensor(T.t4[:], T.t3[:], T.t2[:, 2, :], A.add))
     Ds, SM = T.t4[:, 0:2], T.t4[:, 2:4]
     wv(e_t4)
-    e_nh = ev(V.tensor_scalar(sm(9), Ds, -float(D) / 12.0, None, A.mult))
     e_h = ev(V.tensor_scalar(sm(8), Ds, 1.0 / 12.0, None, A.mult))
 
     ws(e_d)
@@ -220,39 +222,38 @@ def rank_program(g, core, T, topo):
     wv(*e_q1)
     e_e1 = ev(V.tensor_tensor(sm(3), SM, sm(0), A.add))
     wv(e_e1, e_t)
-    e_vr = ev(V.tensor_tensor(sm(4), sm(3), sm(2), A.subtract))
-    wv(e_vr)
-    e_vp = ev(V.tensor_scalar(sm(6), sm(4), float(D * EPS), None, A.add))
-    wv(e_vp)
-    e_r2 = ev(V.reciprocal(sm(7), sm(6)))
-    wv(e_r2, e_pd)
-    e_a1 = ev(V.tensor_tensor(sm(17), sm(16), sm(7), A.mult))
+    e_nv = ev(V.tensor_tensor(sm(4), sm(2), sm(3), A.subtract))
+    wv(e_nv)
+    e_r2 = ev(V.reciprocal(sm(7), sm(4)))
 
-    ws(e_nh)
-    e_er = [ev(S.activation(T.er[:, :, b], GX[:, :, b], F.Identity, bias=smc(9, b), scale=float(D)))
-            for b in range(2)]
     ws(e_h)
-    e_xh = [ev(S.activation(T.xh[:, bs(b)], T.xc[:, bs(b)], F.Identity, bias=smc(8, b))) for b in range(2)]
-    ws(e_vr, e_ri, e_bc)
-    e_sq = [ev(S.activation(smc(5, b), smc(4, b), F.Sqrt, bias=smc(15, b), scale=smc(14, b)))
+    e_er = [ev(S.activation(T.er[:, :, b], GX[:, :, b], F.Identity, bias=smc(8, b), scale=-1.0))
             for b in range(2)]
+
+    def root(b):
+        ws(e_nv, e_nri, e_pdn)
+        e_sq = ev(S.activation(smc(5, b), smc(4, b), F.Sqrt, scale=smc(15, b)))
+        ws(e_sq)
+        return ev(S.activation(smc(18, b), smc(5, b), F.Identity, scale=smc(19, b)))
 
     def diag(b):
-        ws(e_a1, e_sq[b])
-        e_rs = ev(S.activation(smc(18, b), smc(5, b), F.Identity, scale=smc(17, b)))
-        ws(e_rs, e_id)
-        return ev(S.activation(T.dg[:, bs(b)], T.ident[:], F.Identity, scale=smc(18, b)))
+        wv(e_r2, e_rt[b], e_id)
+        return ev(V.tensor_scalar(T.dg[:, bs(b)], T.ident[:], smc(7, b), smc(18, b), A.mult, A.mult))
 
+    e_rt = [root(0)]
+    ws(*e_xc)
+    e_xh = [ev(S.activation(T.xh[:, bs(b)], T.xc[:, bs(b)], F.Identity, bias=smc(8, b))) for b in range(2)]
+    e_rt.append(root(1))
     e_dg = [diag(0)]
+
     ws(*owny)
     S.wait_ge(T.sem.ay1, n_a1)
     S.wait_ge(T.sem.ay2, n_a2)
     e_dn = []
     for b in range(2):
-        e_na = ev(S.activation(T.jq[:, 2 + b, :], GY[:, :, b], F.Copy, scale=-1.0, accum_out=smc(11, b)))
+        e_na = ev(S.activation(T.jq[:, 2 + b, :], GY[:, :, b], F.Copy, scale=-1.0 / D, accum_out=smc(11, b)))
         ws(e_na, e_pr[b])
         e_dn.append(ev(S.activation(dT[b], dT[b], F.Identity, bias=smc(11, b))))
-    e_dg.append(diag(1))
 
     wv(*owny)
     wv(*e_er)
@@ -268,6 +269,8 @@ def rank_program(g, core, T, topo):
                                  A.mult, A.mult))
         wv(e_a, e_dn[b])
         e_w.append(ev(V.tensor_tensor(T.w[:, bs(b)], T.tmp[:, bs(b)], dT[b], A.add)))
+        if b == 0:
+            e_dg.append(diag(1))
 
     pieces = [(0, T.o0, 0, 128), (1, T.o1, 128, 64), (1, T.o2, 192, 64)]
     e_o = []

@@ -14,14 +14,13 @@ SCRATCH = {
     "ident": ("sbuf", [128, 128], "float32"),
     "GX": ("sbuf", [128, N, 4], "float32"),
     "GY": ("sbuf", [128, N, 4], "float32"),
-    "urep": ("sbuf", [128, N, 2], "float32"),
+    "zz": ("sbuf", [128, N], "float32"),
+    "dd": ("sbuf", [128, 2, N], "float32"),
+    "scm": ("sbuf", [128, 2, N], "float32"),
+    "idp": ("sbuf", [128, 256], "float32"),
     "er": ("sbuf", [128, N, 2], "float32"),
     "p2": ("sbuf", [128, N, 2], "float32"),
     "sc": ("sbuf", [128, 2, N], "float32"),
-    "t1": ("sbuf", [128, 6, 4], "float32"),
-    "t2": ("sbuf", [128, 3, 4], "float32"),
-    "t3": ("sbuf", [128, 4], "float32"),
-    "t4": ("sbuf", [128, 4], "float32"),
     "sm": ("sbuf", [128, 88], "float32"),
     "jq": ("sbuf", [128, 4, N], "float32"),
     "junk": ("sbuf", [128, 6, 128], "float32"),
@@ -138,7 +137,7 @@ def rank_program(g, core, T, topo):
     e_x = ev(Y.dma_start(T.xs[:], T.x[:]), 16)
     e_dy = ev(S.dma_start(T.dys[:], T.dy[:]), 16)
     e_ones = ev(V.memset(T.ones[:], 1.0))
-    e_z = ev(V.memset(T.urep[:], 0.0))
+    e_z = ev(V.memset(T.zz[:], 0.0))
     wg(e_ones)
     e_id = ev(g.affine_select(T.ident[:], T.ones[:], [[-1, 128]], A.is_equal, 0.0, 0, 1))
 
@@ -164,9 +163,11 @@ def rank_program(g, core, T, topo):
         wv(e_dT[b], e_xc[b])
         e_pr.append(ev(V.tensor_tensor(T.pr[:, bs(b)], T.xc[:, bs(b)], dT[b], A.mult)))
         wv(e_pr[b])
-        e_c.append(ev(V.tensor_reduce(GY[:, me, 2 + b:3 + b], T.pr[:, bs(b)], AxisListType.X, A.add)))
+        e_c.append(ev(V.tensor_reduce(GY[:, me, 2 + b:3 + b], T.pr[:, bs(b)], AxisListType.X, A.add,
+                                      negate=True)))
         ws(e_dT[b], e_pr[b])
-        e_sd.append(ev(S.activation(T.junk[:, 4 + b, :], dT[b], F.Copy, accum_out=GY[:, me, b:b + 1])))
+        e_sd.append(ev(S.activation(T.junk[:, 4 + b, :], dT[b], F.Copy, scale=-1.0 / 12.0,
+                                    accum_out=GY[:, me, b:b + 1])))
     ownx = e_u + e_m2
     owny = e_sd + e_c
 
@@ -179,79 +180,64 @@ def rank_program(g, core, T, topo):
     g.wait_ge(T.sem.ay1, n_a1)
     hop2(GY, T.sem.ay2, T.sem.senty)
 
-    e_ur = []
-    for b in range(2):
-        wv(e_z, e_u[b])
-        e_ur.append(ev(V.tensor_scalar(T.urep[:, :, b], T.urep[:, :, b], GX[:, me, b:b + 1], None, A.add)))
+    wv(*e_u)
+    e_mo = ev(V.tensor_scalar(sm(20), GX[:, me, 0:2], -1.0, None, A.mult))
     wv(*e_m2)
     e_vo = ev(V.tensor_scalar(sm(13), GX[:, me, 2:4], float(D * EPS), None, A.add))
     ws(e_vo)
     e_pd = ev(S.activation(sm(16), sm(13), F.Sqrt, scale=float(D)))
     wv(e_vo)
     e_ri = ev(V.reciprocal(sm(14), sm(13)))
-    wv(e_ri)
-    e_nri = ev(V.tensor_scalar(sm(15), sm(14), -1.0, None, A.mult))
-    wv(e_pd)
-    e_pdn = ev(V.tensor_scalar(sm(19), sm(16), -1.0, None, A.mult))
-    V.wait_ge(T.sem.sentx, n_sent)
-    e_own = ev(V.tensor_copy(GX[:, me, 2:4], sm(13)))
+    wv(e_pd, e_id)
+    e_ip = [ev(V.tensor_scalar(T.idp[:, bs(b)], T.ident[:], smc(16, b), None, A.mult)) for b in range(2)]
+
+    ws(*ownx)
+    ws(e_mo)
+    S.wait_ge(T.sem.ax1, n_a1)
+    S.wait_ge(T.sem.ax2, n_a2)
+    e_d = [ev(S.activation(T.dd[:, b, :], GX[:, :, b], F.Identity, bias=smc(20, b), accum_out=smc(0, b)))
+           for b in range(2)]
+    e_q = []
+    for b in range(2):
+        ws(e_d[b])
+        e_q.append(ev(S.activation(T.jq[:, b, :], T.dd[:, b, :], F.Square, scale=math.sqrt(128.0),
+                                   accum_out=smc(1, b))))
+    e_t = ev(S.activation(sm(2), sm(0), F.Square, scale=math.sqrt(128.0 / 12.0)))
 
     wv(*ownx)
-    wv(*e_ur)
-    wv(e_own)
+    wv(e_z)
     V.wait_ge(T.sem.ax1, n_a1)
     V.wait_ge(T.sem.ax2, n_a2)
-    e_d = ev(V.tensor_tensor(GX[:, :, 0:2], GX[:, :, 0:2], T.urep[:], A.subtract))
-    wv(e_d)
-    e_t1 = ev(V.tensor_tensor(T.t1[:], GX[:, 0:6, :], GX[:, 6:12, :], A.add))
-    wv(e_t1)
-    e_t2 = ev(V.tensor_tensor(T.t2[:], T.t1[:, 0:3, :], T.t1[:, 3:6, :], A.add))
-    wv(e_t2)
-    e_t3 = ev(V.tensor_tensor(T.t3[:], T.t2[:, 0, :], T.t2[:, 1, :], A.add))
-    wv(e_t3)
-    e_t4 = ev(V.tensor_tensor(T.t4[:], T.t3[:], T.t2[:, 2, :], A.add))
-    Ds, SM = T.t4[:, 0:2], T.t4[:, 2:4]
-    wv(e_t4)
-    e_h = ev(V.tensor_scalar(sm(8), Ds, 1.0 / 12.0, None, A.mult))
-
-    ws(e_d)
-    e_q1 = [ev(S.activation(T.jq[:, b, :], GX[:, :, b], F.Square, scale=math.sqrt(128.0),
-                            accum_out=smc(0, b))) for b in range(2)]
-    ws(e_t4)
-    e_t = ev(S.activation(sm(2), Ds, F.Square, scale=math.sqrt(128.0 / 12.0)))
-    wv(*e_q1)
-    e_e1 = ev(V.tensor_tensor(sm(3), SM, sm(0), A.add))
-    wv(e_e1, e_t)
-    e_nv = ev(V.tensor_tensor(sm(4), sm(2), sm(3), A.subtract))
-    wv(e_nv)
-    e_r2 = ev(V.reciprocal(sm(7), sm(4)))
-
-    ws(e_h)
-    e_er = [ev(S.activation(T.er[:, :, b], GX[:, :, b], F.Identity, bias=smc(8, b), scale=-1.0))
+    e_sm = [ev(V.tensor_tensor_scan(T.scm[:, b, :], GX[:, :, 2 + b], T.zz[:], float(D * EPS), A.add, A.add))
             for b in range(2)]
-
-    def root(b):
-        ws(e_nv, e_nri, e_pdn)
-        e_sq = ev(S.activation(smc(5, b), smc(4, b), F.Sqrt, scale=smc(15, b)))
-        ws(e_sq)
-        return ev(S.activation(smc(18, b), smc(5, b), F.Identity, scale=smc(19, b)))
-
-    def diag(b):
-        wv(e_r2, e_rt[b], e_id)
-        return ev(V.tensor_scalar(T.dg[:, bs(b)], T.ident[:], smc(7, b), smc(18, b), A.mult, A.mult))
-
-    e_rt = [root(0)]
-    ws(*e_xc)
+    e_er = []
+    for b in range(2):
+        wv(e_d[b])
+        e_er.append(ev(V.tensor_scalar(T.er[:, :, b], T.dd[:, b, :], -12.0, smc(0, b), A.mult, A.add)))
+    e_h = ev(V.tensor_scalar(sm(8), sm(0), 1.0 / 12.0, None, A.mult))
+    e_vp = []
+    for b in range(2):
+        wv(e_q[b], e_t, e_sm[b])
+        e_vp.append(ev(V.tensor_scalar(smc(4, b), smc(1, b), T.scm[:, b, N - 1:N], smc(2, b), A.add, A.subtract)))
+    wv(*e_vp)
+    e_r2 = ev(V.reciprocal(sm(7), sm(4)))
+    e_sq = []
+    for b in range(2):
+        ws(e_vp[b], e_ri)
+        e_sq.append(ev(S.activation(smc(5, b), smc(4, b), F.Sqrt, scale=smc(14, b))))
+    e_dg = []
+    for b in range(2):
+        wv(e_r2, e_sq[b], e_ip[b])
+        e_dg.append(ev(V.tensor_scalar(T.dg[:, bs(b)], T.idp[:, bs(b)], smc(7, b), smc(5, b), A.mult, A.mult)))
+    ws(e_h, *e_xc)
     e_xh = [ev(S.activation(T.xh[:, bs(b)], T.xc[:, bs(b)], F.Identity, bias=smc(8, b))) for b in range(2)]
-    e_rt.append(root(1))
-    e_dg = [diag(0)]
 
     ws(*owny)
     S.wait_ge(T.sem.ay1, n_a1)
     S.wait_ge(T.sem.ay2, n_a2)
     e_dn = []
     for b in range(2):
-        e_na = ev(S.activation(T.jq[:, 2 + b, :], GY[:, :, b], F.Copy, scale=-1.0 / D, accum_out=smc(11, b)))
+        e_na = ev(S.activation(T.jq[:, 2 + b, :], GY[:, :, b], F.Copy, scale=12.0 / D, accum_out=smc(11, b)))
         ws(e_na, e_pr[b])
         e_dn.append(ev(S.activation(dT[b], dT[b], F.Identity, bias=smc(11, b))))
 
@@ -261,16 +247,14 @@ def rank_program(g, core, T, topo):
     V.wait_ge(T.sem.ay2, n_a2)
     e_p2 = ev(V.tensor_tensor(T.p2[:], T.er[:], GY[:, :, 0:2], A.mult))
     wv(e_p2)
+    e_cv = [ev(V.tensor_tensor_scan(T.sc[:, b, :], T.p2[:, :, b], GY[:, :, 2 + b], 0.0, A.add, A.add)) for b in range(2)]
     e_w = []
     for b in range(2):
-        e_cv = ev(V.tensor_tensor_scan(T.sc[:, b, :], T.p2[:, :, b], GY[:, :, 2 + b], 0.0, A.add, A.add))
-        wv(e_cv, e_xh[b])
+        wv(e_cv[b], e_xh[b], e_r2)
         e_a = ev(V.tensor_scalar(T.tmp[:, bs(b)], T.xh[:, bs(b)], smc(7, b), T.sc[:, b, N - 1:N],
                                  A.mult, A.mult))
         wv(e_a, e_dn[b])
         e_w.append(ev(V.tensor_tensor(T.w[:, bs(b)], T.tmp[:, bs(b)], dT[b], A.add)))
-        if b == 0:
-            e_dg.append(diag(1))
 
     pieces = [(0, T.o0, 0, 128), (1, T.o1, 128, 64), (1, T.o2, 192, 64)]
     e_o = []
@@ -291,6 +275,7 @@ def rank_program(g, core, T, topo):
     e_s2 = ev(S.dma_start(T.dx[:, c0:c0 + n], T.dxs[:, c0:c0 + n]), 16)
     wy(*e_st)
     ws(e_s2)
+    g.wait_ge(T.sem.sentx, n_sent)
     g.wait_ge(T.sem.senty, n_sent)
     for e in events:
         if e[0] not in seen:

@@ -11,6 +11,8 @@ SCRATCH = {
     "xs": ("sbuf", [128, 256], "float32"),
     "dys": ("sbuf", [128, 256], "float32"),
     "ones": ("sbuf", [128, 128], "float32"),
+    "c1": ("sbuf", [128, 128], "float32"),
+    "aug": ("sbuf", [128, 132], "float32"),
     "ident": ("sbuf", [128, 128], "float32"),
     "GX": ("sbuf", [128, N, 4], "float32"),
     "GY": ("sbuf", [128, N, 4], "float32"),
@@ -131,34 +133,37 @@ def rank_program(g, core, T, topo):
                               srcs=[pair], dsts=[pair for _ in chip_peers], alu_op=0),
         ], local_sem=sent)
 
-    xT = [T.xT0[:, 0:128], T.xT1[:, 0:128]]
+    xP = [T.xT0, T.xT1]
     dT = [T.dT0[:, 0:128], T.dT1[:, 0:128]]
 
-    e_x = ev(Y.dma_start(T.xs[:], T.x[:]), 16)
-    e_dy = ev(S.dma_start(T.dys[:], T.dy[:]), 16)
+    e_x = [ev(Y.dma_start(T.xs[:, bs(0)], T.x[:, bs(0)]), 16),
+           ev(S.dma_start(T.xs[:, bs(1)], T.x[:, bs(1)]), 16)]
+    e_dy = ev(Y.dma_start(T.dys[:], T.dy[:]), 16)
+    e_c1 = ev(V.memset(T.c1[:], 127.0 / 128.0))
+    e_nc = ev(V.memset(T.aug[:, 128:129], -1.0 / 128.0))
     e_ones = ev(V.memset(T.ones[:], 1.0))
     e_z = ev(V.memset(T.zz[:], 0.0))
+    wg(e_c1)
+    e_cen = ev(g.affine_select(T.aug[:, 0:128], T.c1[:], [[-1, 128]], A.is_equal, -1.0 / 128.0, 0, 1))
     wg(e_ones)
     e_id = ev(g.affine_select(T.ident[:], T.ones[:], [[-1, 128]], A.is_equal, 0.0, 0, 1))
 
     e_xT, e_dT = [], []
     for b in range(2):
-        wp(e_x, e_id)
-        e_xT.append(ev(P.transpose(xT[b], T.xs[:, bs(b)], T.ident[:])))
+        wp(e_x[b], e_cen, e_nc)
+        e_xT.append(ev(P.matmul(xP[b][:, 0:129], T.xs[:, bs(b)], T.aug[:, 0:129], True, True)))
     for b in range(2):
-        wp(e_dy)
+        wp(e_dy, e_id)
         e_dT.append(ev(P.transpose(dT[b], T.dys[:, bs(b)], T.ident[:])))
 
     e_u, e_xc, e_m2, e_pr, e_c, e_sd = [], [], [], [], [], []
     for b in range(2):
         ws(e_xT[b])
-        e_u.append(ev(S.activation(T.junk[:, b, :], xT[b], F.Copy, scale=-1.0 / 128.0,
-                                   accum_out=GX[:, me, b:b + 1])))
-        ws(e_u[b])
-        e_m2.append(ev(S.activation(T.junk[:, 2 + b, :], xT[b], F.Square, bias=GX[:, me, b:b + 1],
+        e_m2.append(ev(S.activation(T.junk[:, 2 + b, :], xP[b][:, 0:128], F.Square,
                                     accum_out=GX[:, me, 2 + b:3 + b])))
+        e_u.append(ev(S.activation(GX[:, me, b:b + 1], xP[b][:, 128:129], F.Copy)))
         wv(e_xT[b], e_u[b], e_m2[b])
-        e_xc.append(ev(V.tensor_scalar(T.xc[:, bs(b)], xT[b], GX[:, me, b:b + 1], None, A.add)))
+        e_xc.append(ev(V.tensor_copy(T.xc[:, bs(b)], xP[b][:, 0:128])))
     for b in range(2):
         wv(e_dT[b], e_xc[b])
         e_pr.append(ev(V.tensor_tensor(T.pr[:, bs(b)], T.xc[:, bs(b)], dT[b], A.mult)))

import math
from concourse.bass import DstId, RemoteDMATransfer
from concourse.mybir import AluOpType, AxisListType, ActivationFunctionType

N = 12
D = 128 * N
EPS = 0.01
NSEM = 90

SCRATCH = {
    "xs": ("sbuf", [128, 256], "float32"),
    "dys": ("sbuf", [128, 256], "float32"),
    "ones": ("sbuf", [128, 128], "float32"),
    "c1": ("sbuf", [128, 128], "float32"),
    "aug": ("sbuf", [128, 132], "float32"),
    "ident": ("sbuf", [128, 128], "float32"),
    "GX": ("sbuf", [128, N, 4], "float32"),
    "GY": ("sbuf", [128, N, 4], "float32"),
    "zz": ("sbuf", [128, N], "float32"),
    "dd": ("sbuf", [128, 2, N], "float32"),
    "scm": ("sbuf", [128, 2, N], "float32"),
    "idp": ("sbuf", [128, 256], "float32"),
    "er": ("sbuf", [128, N, 2], "float32"),
    "p2": ("sbuf", [128, N, 2], "float32"),
    "sc": ("sbuf", [128, 2, N], "float32"),
    "sm": ("sbuf", [128, 88], "float32"),
    "jq": ("sbuf", [128, 4, N], "float32"),
    "junk": ("sbuf", [128, 6, 128], "float32"),
    "xc": ("sbuf", [128, 256], "float32"),
    "xh": ("sbuf", [128, 256], "float32"),
    "pr": ("sbuf", [128, 256], "float32"),
    "tmp": ("sbuf", [128, 256], "float32"),
    "w": ("sbuf", [128, 256], "float32"),
    "dg": ("sbuf", [128, 256], "float32"),
    "dxs": ("sbuf", [128, 256], "float32"),
    "xT0": ("psum", [128, 512], "float32"),
    "xT1": ("psum", [128, 512], "float32"),
    "dT0": ("psum", [128, 512], "float32"),
    "dT1": ("psum", [128, 512], "float32"),
    "o0": ("psum", [128, 512], "float32"),
    "o1": ("psum", [128, 512], "float32"),
    "o2": ("psum", [128, 512], "float32"),
}
SEMAPHORES = ["ax1", "ax2", "ay1", "ay2", "sentx", "senty"] + ["s%d" % i for i in range(NSEM)]


def _bits(m):
    return bin(m).count("1")


def rank_program(g, core, T, topo):
    rank = T.rank_of(core)
    if rank is None:
        return
    A, F = AluOpType, ActivationFunctionType
    V, S, P, Y = g.vector, g.scalar, g.tensor, g.sync
    GX, GY = T.GX, T.GY

    cnt = [0]
    events = []
    seen = {}

    def ev(instr, val=1):
        e = (cnt[0], T.sem["s%d" % cnt[0]], val)
        cnt[0] += 1
        instr.then_inc(e[1], val)
        events.append(e)
        return e

    def wait(qname, q, *es):
        for e in es:
            if (qname, e[0]) not in seen:
                seen[(qname, e[0])] = True
                seen[e[0]] = True
                q.wait_ge(e[1], e[2])

    def wv(*es): wait("v", V, *es)
    def ws(*es): wait("s", S, *es)
    def wp(*es): wait("p", P, *es)
    def wy(*es): wait("y", Y, *es)
    def wg(*es): wait("g", g, *es)

    cores = list(T.cores)
    my_host = topo.host(core)
    chip_peers = [c for c in cores if c != core and topo.host(c) == my_host and topo.chip(c) == topo.chip(core)]
    rack_peers = [c for c in cores if topo.host(c) != my_host and topo.rack(topo.host(c)) == topo.rack(my_host)]

    def far_of(c):
        pos = [k for k in cores if topo.host(k) == topo.host(c)].index(c)
        return [k for k in cores if topo.rack(topo.host(k)) != topo.rack(topo.host(c)) and topo.may_write(c, k)][pos]

    far_peer = far_of(core)
    order = []
    for c in cores:
        if c not in order:
            order.append(c)
            order.append(far_of(c))
    me = order.index(core)
    lo = min(me, order.index(far_peer))
    m_off = topo.mask(core, rack_peers[0]) & topo.mask(core, far_peer)
    m_on = topo.mask(core, chip_peers[0]) & ~m_off
    n_a1 = _bits(m_off)
    n_a2 = len(rack_peers) * _bits(m_off) + len(chip_peers) * _bits(m_on)
    n_sent = 2 * _bits(m_off) + _bits(m_on)

    def bs(b):
        return slice(b * 128, (b + 1) * 128)

    def sm(k, n=2):
        return T.sm[:, 4 * k:4 * k + n]

    def smc(k, b):
        return T.sm[:, 4 * k + b:4 * k + b + 1]

    def ids(cs):
        out = []
        for c in cs:
            rid, pid = topo.addr(c, core)
            out.append(DstId(rid=rid, pnc=pid))
        return out

    def hop1(buf, arrive, sent):
        rid, pid = topo.addr(far_peer, core)
        slot = buf[:, me, :]
        g.remote_dma(slot, slot, arrive, sent, pid, rid, m_off)

    def hop2(buf, arrive, sent):
        pair = buf[:, lo:lo + 2, :]
        g.remote_dma_fused([
            RemoteDMATransfer(dst_ids=ids(rack_peers), dma_engine_mask=m_off, remote_sem=arrive,
                              srcs=[pair], dsts=[pair for _ in rack_peers], alu_op=0),
            RemoteDMATransfer(dst_ids=ids(chip_peers), dma_engine_mask=m_on, remote_sem=arrive,
                              srcs=[pair], dsts=[pair for _ in chip_peers], alu_op=0),
        ], local_sem=sent)

    xP = [T.xT0, T.xT1]
    dT = [T.dT0[:, 0:128], T.dT1[:, 0:128]]

    e_x = [ev(Y.dma_start(T.xs[:, bs(0)], T.x[:, bs(0)]), 16),
           ev(S.dma_start(T.xs[:, bs(1)], T.x[:, bs(1)]), 16)]
    e_dy = ev(Y.dma_start(T.dys[:], T.dy[:]), 16)
    e_c1 = ev(V.memset(T.c1[:], 127.0 / 128.0))
    e_nc = ev(V.memset(T.aug[:, 128:129], -1.0 / 128.0))
    e_ones = ev(V.memset(T.ones[:], 1.0))
    e_z = ev(V.memset(T.zz[:], 0.0))
    wg(e_c1)
    e_cen = ev(g.affine_select(T.aug[:, 0:128], T.c1[:], [[-1, 128]], A.is_equal, -1.0 / 128.0, 0, 1))
    wg(e_ones)
    e_id = ev(g.affine_select(T.ident[:], T.ones[:], [[-1, 128]], A.is_equal, 0.0, 0, 1))

    e_xT, e_dT = [], []
    for b in range(2):
        wp(e_x[b], e_cen, e_nc)
        e_xT.append(ev(P.matmul(xP[b][:, 0:129], T.xs[:, bs(b)], T.aug[:, 0:129], True, True)))
    for b in range(2):
        wp(e_dy, e_id)
        e_dT.append(ev(P.transpose(dT[b], T.dys[:, bs(b)], T.ident[:])))

    e_u, e_xc, e_m2, e_pr, e_c, e_sd = [], [], [], [], [], []
    for b in range(2):
        ws(e_xT[b])
        e_m2.append(ev(S.activation(T.junk[:, 2 + b, :], xP[b][:, 0:128], F.Square,
                                    accum_out=GX[:, me, 2 + b:3 + b])))
        e_u.append(ev(S.activation(GX[:, me, b:b + 1], xP[b][:, 128:129], F.Copy)))
        wv(e_xT[b], e_u[b], e_m2[b])
        e_xc.append(ev(V.tensor_copy(T.xc[:, bs(b)], xP[b][:, 0:128])))
    for b in range(2):
        wv(e_dT[b], e_xc[b])
        e_pr.append(ev(V.tensor_tensor(T.pr[:, bs(b)], T.xc[:, bs(b)], dT[b], A.mult)))
        wv(e_pr[b])
        e_c.append(ev(V.tensor_reduce(GY[:, me, 2 + b:3 + b], T.pr[:, bs(b)], AxisListType.X, A.add,
                                      negate=True)))
        ws(e_dT[b], e_pr[b])
        e_sd.append(ev(S.activation(T.junk[:, 4 + b, :], dT[b], F.Copy, scale=-1.0 / 12.0,
                                    accum_out=GY[:, me, b:b + 1])))
    ownx = e_u + e_m2
    owny = e_sd + e_c

    wg(*ownx)
    hop1(GX, T.sem.ax1, T.sem.sentx)
    wg(*owny)
    hop1(GY, T.sem.ay1, T.sem.senty)
    g.wait_ge(T.sem.ax1, n_a1)
    hop2(GX, T.sem.ax2, T.sem.sentx)
    g.wait_ge(T.sem.ay1, n_a1)
    hop2(GY, T.sem.ay2, T.sem.senty)

    wv(*e_u)
    e_mo = ev(V.tensor_scalar(sm(20), GX[:, me, 0:2], -1.0, None, A.mult))
    wv(*e_m2)
    e_vo = ev(V.tensor_scalar(sm(13), GX[:, me, 2:4], float(D * EPS), None, A.add))
    ws(e_vo)
    e_pd = ev(S.activation(sm(16), sm(13), F.Sqrt, scale=float(D)))
    wv(e_vo)
    e_ri = ev(V.reciprocal(sm(14), sm(13)))
    wv(e_pd, e_id)
    e_ip = [ev(V.tensor_scalar(T.idp[:, bs(b)], T.ident[:], smc(16, b), None, A.mult)) for b in range(2)]

    ws(*ownx)
    ws(e_mo)
    S.wait_ge(T.sem.ax1, n_a1)
    S.wait_ge(T.sem.ax2, n_a2)
    e_d = [ev(S.activation(T.dd[:, b, :], GX[:, :, b], F.Identity, bias=smc(20, b), accum_out=smc(0, b)))
           for b in range(2)]
    e_q = []
    for b in range(2):
        ws(e_d[b])
        e_q.append(ev(S.activation(T.jq[:, b, :], T.dd[:, b, :], F.Square, scale=math.sqrt(128.0),
                                   accum_out=smc(1, b))))
    e_t = ev(S.activation(sm(2), sm(0), F.Square, scale=math.sqrt(128.0 / 12.0)))

    wv(*ownx)
    wv(e_z)
    V.wait_ge(T.sem.ax1, n_a1)
    V.wait_ge(T.sem.ax2, n_a2)
    e_sm = [ev(V.tensor_tensor_scan(T.scm[:, b, :], GX[:, :, 2 + b], T.zz[:], float(D * EPS), A.add, A.add))
            for b in range(2)]
    e_er = []
    for b in range(2):
        wv(e_d[b])
        e_er.append(ev(V.tensor_scalar(T.er[:, :, b], T.dd[:, b, :], -12.0, smc(0, b), A.mult, A.add)))
    e_h = ev(V.tensor_scalar(sm(8), sm(0), 1.0 / 12.0, None, A.mult))
    e_vp = []
    for b in range(2):
        wv(e_q[b], e_t, e_sm[b])
        e_vp.append(ev(V.tensor_scalar(smc(4, b), smc(1, b), T.scm[:, b, N - 1:N], smc(2, b), A.add, A.subtract)))
    wv(*e_vp)
    e_r2 = ev(V.reciprocal(sm(7), sm(4)))
    e_sq = []
    for b in range(2):
        ws(e_vp[b], e_ri)
        e_sq.append(ev(S.activation(smc(5, b), smc(4, b), F.Sqrt, scale=smc(14, b))))
    e_dg = []
    for b in range(2):
        wv(e_r2, e_sq[b], e_ip[b])
        e_dg.append(ev(V.tensor_scalar(T.dg[:, bs(b)], T.idp[:, bs(b)], smc(7, b), smc(5, b), A.mult, A.mult)))
    ws(e_h, *e_xc)
    e_xh = [ev(S.activation(T.xh[:, bs(b)], T.xc[:, bs(b)], F.Identity, bias=smc(8, b))) for b in range(2)]

    ws(*owny)
    S.wait_ge(T.sem.ay1, n_a1)
    S.wait_ge(T.sem.ay2, n_a2)
    e_dn = []
    for b in range(2):
        e_na = ev(S.activation(T.jq[:, 2 + b, :], GY[:, :, b], F.Copy, scale=12.0 / D, accum_out=smc(11, b)))
        ws(e_na, e_pr[b])
        e_dn.append(ev(S.activation(dT[b], dT[b], F.Identity, bias=smc(11, b))))

    wv(*owny)
    wv(*e_er)
    V.wait_ge(T.sem.ay1, n_a1)
    V.wait_ge(T.sem.ay2, n_a2)
    e_p2 = ev(V.tensor_tensor(T.p2[:], T.er[:], GY[:, :, 0:2], A.mult))
    wv(e_p2)
    e_cv = [ev(V.tensor_tensor_scan(T.sc[:, b, :], T.p2[:, :, b], GY[:, :, 2 + b], 0.0, A.add, A.add)) for b in range(2)]
    e_w = []
    for b in range(2):
        wv(e_cv[b], e_xh[b], e_r2)
        e_a = ev(V.tensor_scalar(T.tmp[:, bs(b)], T.xh[:, bs(b)], smc(7, b), T.sc[:, b, N - 1:N],
                                 A.mult, A.mult))
        wv(e_a, e_dn[b])
        e_w.append(ev(V.tensor_tensor(T.w[:, bs(b)], T.tmp[:, bs(b)], dT[b], A.add)))

    pieces = [(0, T.o0, 0, 128), (1, T.o1, 128, 64), (1, T.o2, 192, 64)]
    e_o = []
    for b, ob, c0, n in pieces:
        wp(e_w[b], e_dg[b])
        e_o.append(ev(P.matmul(ob[:, 0:n], T.w[:, bs(b)], T.dg[:, c0:c0 + n], True, True)))
    e_st = []
    for k in range(2):
        b, ob, c0, n = pieces[k]
        wv(e_o[k])
        e_cp = ev(V.tensor_copy(T.dxs[:, c0:c0 + n], ob[:, 0:n]))
        wy(e_cp)
        e_st.append(ev(Y.dma_start(T.dx[:, c0:c0 + n], T.dxs[:, c0:c0 + n]), 16))
    b, ob, c0, n = pieces[2]
    ws(e_o[2])
    e_cp = ev(S.activation(T.dxs[:, c0:c0 + n], ob[:, 0:n], F.Copy))
    ws(e_cp)
    e_s2 = ev(S.dma_start(T.dx[:, c0:c0 + n], T.dxs[:, c0:c0 + n]), 16)
    wy(*e_st)
    ws(e_s2)
    g.wait_ge(T.sem.sentx, n_sent)
    g.wait_ge(T.sem.senty, n_sent)
    for e in events:
        if e[0] not in seen:
            wg(e)
